import numpy as np
import ml_dtypes


def mxq(x, axis, fmt="e4m3"):
    dtype, down = {"e4m3": (ml_dtypes.float8_e4m3fn, 7), "e5m2": (ml_dtypes.float8_e5m2, 14)}[fmt]
    v = np.moveaxis(np.asarray(x, np.float32).astype(ml_dtypes.bfloat16).astype(np.float64), axis, -1)
    blocks = v.reshape(v.shape[:-1] + (-1, 32))
    amax = np.abs(blocks).max(-1, keepdims=True)
    byte = np.maximum(np.where(amax > 0, np.frexp(amax)[1] - 1 + 127, 0) - down, 1)
    scale = np.exp2(byte - 127.0)
    codes = (blocks / scale).astype(np.float32).astype(dtype).astype(np.float64)
    return np.moveaxis((codes * scale).reshape(v.shape), -1, axis)


WIDE = False


def mx_kscale(k):
    if not WIDE:
        return np.ones(k)
    levels = np.array([10, -10, 5, -5, 0])
    if k % 512:
        return np.exp2(np.random.permutation(np.resize(levels, k // 32))).repeat(32)
    a = np.empty((k // 512, 16))
    for p in range(k // 512):
        a[p, :8] = np.random.permutation(np.resize(levels, 8))
        for g in range(8):
            far = levels[np.abs(levels - a[p, g]) >= 10]
            a[p, g + 8] = far[np.random.randint(len(far))]
    return np.exp2(a.ravel()).repeat(32)


def f64(x):
    return np.asarray(x).astype(np.float64)


def striped(idx):
    return np.tile(idx.reshape(-1, 16).T, (8, 1)).astype(np.uint16)


def unstriped(offs):
    return offs[:16].T.reshape(-1).astype(np.int64)


E2M1 = np.array([0.0, 0.5, 1.0, 1.5, 2.0, 3.0, 4.0, 6.0, -0.0, -0.5, -1.0, -1.5, -2.0, -3.0, -4.0, -6.0])


def pack_weight(w, fmt):
    k, n = w.shape
    w = f64(np.asarray(w, np.float32).astype(ml_dtypes.bfloat16)).reshape(k // 32, 32, n)
    amax = np.abs(w).max(1)
    if fmt == "e4m3":
        byte = np.frexp(amax)[1] - 1 + 127 - 7
    else:
        mant, ex = np.frexp(amax / 6.0)
        byte = np.where(mant > 0.5, ex, ex - 1) + 127
    byte = np.clip(np.where(amax > 0, byte, 1), 1, 254)
    scaled = (w * np.exp2(127.0 - byte)[:, None, :]).reshape(k, n).astype(np.float32)
    by_word = np.ascontiguousarray(scaled.reshape(k // 512, 128, 4, n).transpose(0, 1, 3, 2))
    if fmt == "e4m3":
        words = by_word.astype(ml_dtypes.float8_e4m3fn).view(np.uint8)
    else:
        c = by_word.astype(ml_dtypes.float4_e2m1fn).view(np.uint8) & 0xF
        words = (c[..., 0::2] | (c[..., 1::2] << 4)).reshape(k // 512, 128, 2 * n)
    return np.ascontiguousarray(words), np.ascontiguousarray(byte.astype(np.uint8).reshape(k // 512, 16, n))


def unpack_weight(words, scales, fmt):
    g, _, n = scales.shape
    words = np.ascontiguousarray(words).reshape(g, 128, n, -1)
    if fmt == "e4m3":
        vals = words.view(ml_dtypes.float8_e4m3fn).astype(np.float64)
    else:
        nib = np.empty((g, 128, n, 4), np.uint8)
        nib[..., 0::2] = words & 0xF
        nib[..., 1::2] = words >> 4
        vals = E2M1[nib]
    vals = vals * np.repeat(np.exp2(scales.astype(np.float64) - 127.0), 8, axis=1)[..., None]
    return vals.transpose(0, 1, 3, 2).reshape(g * 512, n)


def planes(y):
    n, m = y.shape
    v = y.astype(np.float32).astype(ml_dtypes.bfloat16).astype(np.float64).reshape(n // 32, 32, m)
    top = np.abs(v).max(1)
    byte = np.clip(np.where(top > 0, np.frexp(top)[1] - 1 + 127 - 7, 1), 1, 254)
    codes = (v * np.exp2(127.0 - byte)[:, None, :]).reshape(n, m).astype(np.float32).astype(ml_dtypes.float8_e4m3fn).view(np.uint8)
    words = codes.reshape(n // 512, 128, 4, m).transpose(0, 1, 3, 2)
    return np.ascontiguousarray(words), np.ascontiguousarray(byte.astype(np.uint8).reshape(n // 512, 16, m))


def relu(v):
    return np.maximum(v, 0.0)


K, T, E, C, H, N = 2048, 640, 10, 128, 512, 512


def by_expert(wq, xq):
    return np.concatenate([wq[e].T @ xq[:, e * C:(e + 1) * C] for e in range(E)], axis=1)


def setup_inputs():
    n = np.random.standard_normal
    s = mx_kscale(K)
    u = mx_kscale(H)
    first = np.random.permutation(np.repeat(np.arange(E), T // E))
    second = (first + 1 + np.random.permutation(np.repeat(np.arange(E - 1), -(-T // (E - 1)))[:T])) % E
    while np.bincount(second, minlength=E).max() != T // E:
        load = np.bincount(second, minlength=E); hi, lo = int(load.argmax()), int(load.argmin())
        t = np.flatnonzero((second == hi) & (first != lo))[0]; second[t] = lo
    slot_token = np.empty(E * C, np.int64); pos = np.empty((2, T), np.int64); fill = np.zeros(E, np.int64)
    place = np.stack([np.random.permutation(C) for _ in range(E)])
    for r, deal in enumerate((first, second)):
        for t in np.random.permutation(T):
            e = deal[t]; j = e * C + place[e, fill[e]]; fill[e] += 1; slot_token[j] = t; pos[r, t] = j
    g = np.random.uniform(0.2, 0.8, T)
    x = pack_weight(n((K, T)) * s[:, None], "e4m3")
    return {
        "x_words": x[0],
        "x_scales": x[1],
        "w1": (n((K, H)) / np.sqrt(K) / s[:, None] * u).astype(np.float32),
        "w2": (n((E, H, N)) / np.sqrt(H) / u[None, :, None]).astype(np.float32),
        "gate": np.stack([np.tile(g, (128, 1)), np.tile(1.0 - g, (128, 1))]).astype(np.float32),
        "offs": striped(slot_token),
        "pos1": striped(pos[0]),
        "pos2": striped(pos[1]),
    }


def reference(x_words, x_scales, w1, w2, gate, offs, pos1, pos2):
    w1q = mxq(f64(w1), 0, "e4m3")
    w2q = mxq(f64(w2), 1, "e4m3")
    idx = unstriped(offs)
    x = unpack_weight(x_words, x_scales, "e4m3")
    h = relu(w1q.T @ x)
    y = by_expert(w2q, mxq(h[:, idx], 0, "e4m3"))
    out = sum(f64(gate[r, :1]) * y[:, unstriped(p)] for r, p in enumerate((pos1, pos2)))
    out_0 = out
    return (out_0,) + planes(out_0)

@@ -1,0 +1,284 @@
+from contextlib import ExitStack
+
+import concourse.mybir as mybir
+from concourse.masks import make_identity
+
+K, T, E, C, H, N = 2048, 640, 10, 128, 512, 512
+SLOTS = E * C
+FLOPS = 2 * K * H * T + 2 * H * N * SLOTS
+
+F32 = mybir.dt.float32
+BF16 = mybir.dt.bfloat16
+I32 = mybir.dt.int32
+U32 = mybir.dt.uint32
+U16 = mybir.dt.uint16
+U8 = mybir.dt.uint8
+FP8X4 = mybir.dt.float8_e4m3fn_x4
+MULT = mybir.AluOpType.mult
+ADD = mybir.AluOpType.add
+RELU = mybir.ActivationFunctionType.Relu
+
+P = 128
+PACK = 4
+PASSES = K // (P * PACK)
+PIECE = 256
+HALVES = N // PIECE
+BLOCKS = PIECE // P
+PAIR = 2
+BANK = 512
+TOKEN_CHUNKS = [(0, 256), (256, 256), (512, 128)]
+EXPERT_RUNS = [(0, 4), (4, 4), (8, 2)]
+ON_VECTOR = {(0, 0), (0, 1), (1, 0), (1, 9)}
+BEHIND = {1: 4, 2: 9}
+LAST_ON_SCALAR = {0: 9, 1: 8}
+
+
+def tile_moe_sup_lin_relu_kernel(
+    tc, x_words, x_scales, w1, w2, gate, offs, pos1, pos2, out_0, out_1, out_2
+):
+    nc = tc.nc
+    with ExitStack() as ctx:
+        keep = ctx.enter_context(tc.tile_pool(name="keep", bufs=1))
+        ring = ctx.enter_context(tc.tile_pool(name="ring", bufs=2))
+        psum = ctx.enter_context(tc.psum_pool(name="psum", bufs=1))
+
+        def bank(b):
+            return psum.tile([P, BANK], F32, name="bank%d" % b)
+
+        def held(name, shape, dtype):
+            return keep.tile(shape, dtype, name=name, align_bytes=64)
+
+        def ringed(name, shape, dtype, bufs):
+            return ring.tile(shape, dtype, name=name, bufs=bufs, align_bytes=64)
+
+        def load_piece(rows, name=None):
+            if name is None:
+                raw = ringed("raw", [P, PACK, PIECE], F32, 18)
+            else:
+                raw = held(name, [P, PACK, PIECE], F32)
+            nc.sync.dma_start(out=raw[:], in_=rows.rearrange("(p j) c -> p j c", j=PACK))
+            return raw
+
+        x_planes = held("x_planes", [P, T], U8)
+        nc.vector.memset(x_planes[:].bitcast(I32), 0)
+        for q in range(4):
+            nc.scalar.dma_start(
+                out=x_planes[32 * q : 32 * q + 16, :].bitcast(I32),
+                in_=x_scales[:, 4 * q : 4 * q + 4, :].bitcast(I32),
+            )
+        w1_raw, x_codes = {}, []
+        for g in range(PASSES):
+            for s in range(2):
+                w1_raw[g, s] = load_piece(w1[g * 512 : (g + 1) * 512, s * PIECE : (s + 1) * PIECE])
+            words = held("x_codes%d" % g, [P, T], U32)
+            nc.sync.dma_start(out=words[:].bitcast(I32), in_=x_words[g].rearrange("p t d -> p (t d)").bitcast(I32))
+            x_codes.append(words)
+        slot_tokens = held("slot_tokens", [P, SLOTS // 16], U16)
+        nc.sync.dma_start(slot_tokens[:], offs)
+        w2_raw = {}
+        for e in range(E):
+            w2_raw[0, e] = load_piece(w2[e, :, 0:PIECE], "y0" if e == LAST_ON_SCALAR[0] else None)
+        token_slots = []
+        for r, pos in enumerate((pos1, pos2)):
+            lst = held("token_slots%d" % r, [P, T // 16], U16)
+            nc.sync.dma_start(lst[:], pos)
+            token_slots.append(lst)
+        gates = held("gates", [P, 2, T], F32)
+        nc.sync.dma_start(out=gates[:], in_=gate.rearrange("r p t -> p r t"))
+        for e in range(E):
+            w2_raw[1, e] = load_piece(w2[e, :, PIECE : 2 * PIECE], "y2" if e == LAST_ON_SCALAR[1] else None)
+
+        ident = held("ident", [P, P], F32)
+        make_identity(nc, ident[:])
+
+        wide = [bank(t) for t in range(PACK)]
+        rest = [bank(PACK + t) for t in range(PACK)]
+        for g in range(PASSES):
+            dealt = ringed("w1_dealt", [P, PACK, P, PACK], BF16, 2)
+            for s, copy in enumerate((nc.scalar.copy, nc.vector.tensor_copy)):
+                copy(
+                    out=dealt[:, :, 64 * s : 64 * (s + 1), :].rearrange("p t m j -> p m j t"),
+                    in_=w1_raw[g, s][:].rearrange("p j (m t) -> p m j t", t=PACK),
+                )
+            codes = ringed("w1_codes", [P, H], U32, 2)
+            scales = ringed("w1_scales", [P, H], U8, 2)
+            nc.vector.quantize_mx(
+                out=codes[:].bitcast(FP8X4), scales=scales[:], in_=dealt[:].rearrange("p t m j -> p (t m j)")
+            )
+            for t in (0, 2, 1, 3):
+                for acc, lo, hi in ((wide[t], 0, BANK), (rest[t], BANK, T)):
+                    nc.tensor.matmul_mx(
+                        out=acc[:, 0 : hi - lo],
+                        lhsT=codes[:, t * P : (t + 1) * P].bitcast(FP8X4),
+                        lhsT_scale=scales[:, t * P : (t + 1) * P],
+                        rhs=x_codes[g][:, lo:hi].bitcast(FP8X4),
+                        rhs_scale=x_planes[4 * g : P, lo:hi],
+                        start=(g == 0),
+                        stop=(g == PASSES - 1),
+                    )
+        h_pairs = [held("h_pairs%d" % u, [P, T, PAIR], BF16) for u in range(2)]
+        for t in range(PACK):
+            for acc, lo, hi in ((wide[t], 0, BANK), (rest[t], BANK, T)):
+                dst = h_pairs[t // PAIR][:, lo:hi, t % PAIR]
+                if t < PAIR:
+                    nc.scalar.activation(out=dst, in_=acc[:, 0 : hi - lo], func=RELU)
+                else:
+                    nc.vector.tensor_scalar_max(out=dst, in0=acc[:, 0 : hi - lo], scalar1=0.0)
+
+        h_codes = [held("h_codes%d" % d, [P, 2 * C], U32) for d in range(E // 2)]
+        h_scales = [held("h_scales%d" % d, [P, 2 * C], U8) for d in range(E // 2)]
+
+        def gather_duo(d):
+            picked = ringed("picked", [P, 2, 2 * C], U32, 2)
+            for u in range(2):
+                window = h_pairs[u][:].rearrange("p t e -> p (t e)").bitcast(U32)
+                nc.vector.tensor_copy(out=picked[:, u, :], in_=window.indirect(slot_tokens[:, 16 * d : 16 * (d + 1)]))
+            return picked
+
+        def weave_duo(picked):
+            woven = ringed("woven", [P, 2 * C * PACK], BF16, 2)
+            nc.vector.tensor_copy(
+                out=woven[:].bitcast(I32).rearrange("p (s u) -> p s u", u=2),
+                in_=picked[:].bitcast(I32).rearrange("p u s -> p s u"),
+            )
+            return woven
+
+        def quantise_duo(d, woven):
+            nc.vector.quantize_mx(out=h_codes[d][:].bitcast(FP8X4), scales=h_scales[d][:], in_=woven[:])
+
+        def round_piece(half, e):
+            if half == 1 and e in BEHIND.values():
+                grouped = held("behind%d" % e, [P, PIECE * PACK], BF16)
+            else:
+                grouped = ringed("w2_grouped", [P, PIECE * PACK], BF16, 11)
+            copy = nc.vector.tensor_copy if (half, e) in ON_VECTOR else nc.scalar.copy
+            copy(
+                out=grouped[:].rearrange("p (c i j) -> p c j i", i=4, j=PACK),
+                in_=w2_raw[half, e][:].rearrange("p j (c i) -> p c j i", i=4),
+            )
+            return grouped
+
+        def quantise_piece(grouped):
+            codes = ringed("w2_codes", [P, PIECE], U32, 12)
+            scales = ringed("w2_scales", [P, PIECE], U8, 12)
+            nc.vector.quantize_mx(out=codes[:].bitcast(FP8X4), scales=scales[:], in_=grouped[:])
+            return codes, scales
+
+        y = [held("y%d" % c, [P, SLOTS], F32) for c in range(N // P)]
+        turn = [0]
+
+        def expert_run(half, first, count, pieces):
+            for b in range(BLOCKS):
+                acc = bank(turn[0] % 4)
+                turn[0] = turn[0] + 1
+                for e in range(first, first + count):
+                    codes, scales = pieces[e]
+                    cols = slice((e % 2) * C, (e % 2 + 1) * C)
+                    nc.tensor.matmul_mx(
+                        out=acc[:, (e - first) * C : (e - first + 1) * C],
+                        lhsT=codes[:, b * P : (b + 1) * P].bitcast(FP8X4),
+                        lhsT_scale=scales[:, b * P : (b + 1) * P],
+                        rhs=h_codes[e // 2][:, cols].bitcast(FP8X4),
+                        rhs_scale=h_scales[e // 2][:, cols],
+                        start=True,
+                        stop=True,
+                    )
+                nc.scalar.copy(out=y[half * BLOCKS + b][:, first * C : (first + count) * C], in_=acc[:, 0 : count * C])
+
+        result = [held("result%d" % half, [P, BLOCKS, T], F32) for half in range(HALVES)]
+        by_token = [held("by_token%d" % i, [P, n // P, 2, P, PAIR], BF16) for i, (lo, n) in enumerate(TOKEN_CHUNKS)]
+        out_codes = held("out_codes", [P, T], U32)
+        out_scales = held("out_scales", [P, T], U8)
+
+        def combine(half, i):
+            lo, n = TOKEN_CHUNKS[i]
+            terms = []
+            for r in range(2):
+                if half == 0 and i in BEHIND:
+                    term = held("behind%d" % BEHIND[i], [P, BLOCKS, n], F32) if r == 0 else held("second%d" % i, [P, BLOCKS, n], F32)
+                else:
+                    term = ringed("term%d" % r, [P, BLOCKS, n], F32, 2)
+                for b in range(BLOCKS):
+                    nc.vector.tensor_tensor(
+                        term[:, b, :],
+                        y[half * BLOCKS + b][:].indirect(token_slots[r][:, lo // 16 : (lo + n) // 16]),
+                        gates[:, r, lo : lo + n],
+                        MULT,
+                    )
+                terms.append(term)
+            nc.vector.tensor_tensor(result[half][:, :, lo : lo + n], terms[0][:], terms[1][:], ADD)
+
+        def store_result(half, lo, n):
+            rows = out_0[half * PIECE : (half + 1) * PIECE, lo : lo + n]
+            nc.sync.dma_start(out=rows.rearrange("(b q) t -> q b t", q=P), in_=result[half][:, :, lo : lo + n])
+
+        def turn_to_tokens(half, i):
+            lo, n = TOKEN_CHUNKS[i]
+            acc = bank(2 + 2 * half + i % 2)
+            for kk in range(n // P):
+                for b in range(BLOCKS):
+                    at = (kk * BLOCKS + b) * P
+                    nc.tensor.transpose(acc[:, at : at + P], result[half][:, b, lo + kk * P : lo + (kk + 1) * P], ident[:])
+            nc.scalar.copy(
+                out=by_token[i][:, :, :, 64 * half : 64 * (half + 1), :],
+                in_=acc[:, 0 : n * BLOCKS].rearrange("k (kk p u e) -> k kk u p e", p=64, u=2, e=PAIR),
+            )
+
+        def turn_back(i):
+            lo, n = TOKEN_CHUNKS[i]
+            acc = bank(6 + i % 2)
+            words = by_token[i][:].rearrange("k kk u p e -> k (kk u p e)").bitcast(F32)
+            for at in range(0, 2 * n, P):
+                nc.tensor.transpose(acc[:, at : at + P], words[:, at : at + P], ident[:])
+            rounded = ringed("rounded", [P, n * PACK], BF16, 2)
+            nc.scalar.copy(
+                out=rounded[:].bitcast(F32).rearrange("p (kk r u) -> p kk r u", r=P, u=2),
+                in_=acc[:, 0 : 2 * n].rearrange("p (kk u r) -> p kk r u", r=P, u=2),
+            )
+            nc.vector.quantize_mx(
+                out=out_codes[:, lo : lo + n].bitcast(FP8X4), scales=out_scales[:, lo : lo + n], in_=rounded[:]
+            )
+            nc.sync.dma_start(
+                out=out_1[0].rearrange("p t d -> p (t d)").bitcast(I32)[:, lo : lo + n],
+                in_=out_codes[:, lo : lo + n].bitcast(I32),
+            )
+
+        pieces = {}
+        picked = gather_duo(0)
+        for d in range(E // 2):
+            grouped = [round_piece(0, e) for e in (2 * d, 2 * d + 1)]
+            woven = weave_duo(picked)
+            if d + 1 < E // 2:
+                picked = gather_duo(d + 1)
+            quantise_duo(d, woven)
+            for e in (2 * d, 2 * d + 1):
+                pieces[e] = quantise_piece(grouped[e % 2])
+            for first, count in EXPERT_RUNS:
+                if first + count == 2 * d + 2:
+                    expert_run(0, first, count, pieces)
+
+        pieces = {}
+        for e in range(E):
+            pieces[e] = quantise_piece(round_piece(1, e))
+            for first, count in EXPERT_RUNS:
+                if first + count == e + 1:
+                    expert_run(1, first, count, pieces)
+            if e == 0:
+                combine(0, 0)
+            for i in BEHIND:
+                if BEHIND[i] == e:
+                    combine(0, i)
+        store_result(0, 0, T)
+        for i in range(len(TOKEN_CHUNKS)):
+            turn_to_tokens(0, i)
+
+        for i, (lo, n) in enumerate(TOKEN_CHUNKS):
+            combine(1, i)
+            store_result(1, lo, n)
+            turn_to_tokens(1, i)
+            turn_back(i)
+        for q in range(4):
+            queue = nc.sync if q % 2 == 0 else nc.scalar
+            queue.dma_start(
+                out=out_2[0, 4 * q : 4 * q + 4, :].bitcast(I32), in_=out_scales[32 * q : 32 * q + 4, :].bitcast(I32)
+            )

@@ -28,9 +28,10 @@ PAIR = 2
 BANK = 512
 TOKEN_CHUNKS = [(0, 256), (256, 256), (512, 128)]
 EXPERT_RUNS = [(0, 4), (4, 4), (8, 2)]
-ON_VECTOR = {(0, 0), (0, 1), (1, 0), (1, 9)}
-BEHIND = {1: 4, 2: 9}
-LAST_ON_SCALAR = {0: 9, 1: 8}
+ON_VECTOR = {(1, 0), (1, 1), (1, 9)}
+EARLY_CHUNKS = [(0, 512), (512, 128)]
+WINDOW = 704
+Y_AFTER = {(0, 9): "y0", (0, 8): "y1", (1, 8): "y2", (1, 7): "y3"}
 
 
 def tile_moe_sup_lin_relu_kernel(
@@ -53,7 +54,7 @@ def tile_moe_sup_lin_relu_kernel(
 
         def load_piece(rows, name=None):
             if name is None:
-                raw = ringed("raw", [P, PACK, PIECE], F32, 18)
+                raw = ringed("raw", [P, PACK, PIECE], F32, 16)
             else:
                 raw = held(name, [P, PACK, PIECE], F32)
             nc.sync.dma_start(out=raw[:], in_=rows.rearrange("(p j) c -> p j c", j=PACK))
@@ -70,14 +71,15 @@ def tile_moe_sup_lin_relu_kernel(
         for g in range(PASSES):
             for s in range(2):
                 w1_raw[g, s] = load_piece(w1[g * 512 : (g + 1) * 512, s * PIECE : (s + 1) * PIECE])
-            words = held("x_codes%d" % g, [P, T], U32)
-            nc.sync.dma_start(out=words[:].bitcast(I32), in_=x_words[g].rearrange("p t d -> p (t d)").bitcast(I32))
-            x_codes.append(words)
+            for gx in (g,):
+                words = held("x_codes%d" % gx, [P, T], U32)
+                nc.sync.dma_start(out=words[:].bitcast(I32), in_=x_words[gx].rearrange("p t d -> p (t d)").bitcast(I32))
+                x_codes.append(words)
         slot_tokens = held("slot_tokens", [P, SLOTS // 16], U16)
         nc.sync.dma_start(slot_tokens[:], offs)
         w2_raw = {}
         for e in range(E):
-            w2_raw[0, e] = load_piece(w2[e, :, 0:PIECE], "y0" if e == LAST_ON_SCALAR[0] else None)
+            w2_raw[0, e] = load_piece(w2[e, :, 0:PIECE], Y_AFTER.get((0, e)))
         token_slots = []
         for r, pos in enumerate((pos1, pos2)):
             lst = held("token_slots%d" % r, [P, T // 16], U16)
@@ -86,7 +88,7 @@ def tile_moe_sup_lin_relu_kernel(
         gates = held("gates", [P, 2, T], F32)
         nc.sync.dma_start(out=gates[:], in_=gate.rearrange("r p t -> p r t"))
         for e in range(E):
-            w2_raw[1, e] = load_piece(w2[e, :, PIECE : 2 * PIECE], "y2" if e == LAST_ON_SCALAR[1] else None)
+            w2_raw[1, e] = load_piece(w2[e, :, PIECE : 2 * PIECE], Y_AFTER.get((1, e)))
 
         ident = held("ident", [P, P], F32)
         make_identity(nc, ident[:])
@@ -102,10 +104,14 @@ def tile_moe_sup_lin_relu_kernel(
                 )
             codes = ringed("w1_codes", [P, H], U32, 2)
             scales = ringed("w1_scales", [P, H], U8, 2)
-            nc.vector.quantize_mx(
-                out=codes[:].bitcast(FP8X4), scales=scales[:], in_=dealt[:].rearrange("p t m j -> p (t m j)")
-            )
-            for t in (0, 2, 1, 3):
+            for u in range(2):
+                cols = slice(u * PAIR * P, (u + 1) * PAIR * P)
+                nc.vector.quantize_mx(
+                    out=codes[:, cols].bitcast(FP8X4),
+                    scales=scales[:, cols],
+                    in_=dealt[:, PAIR * u : PAIR * (u + 1)].rearrange("p t m j -> p (t m j)"),
+                )
+            for t in range(PACK):
                 for acc, lo, hi in ((wide[t], 0, BANK), (rest[t], BANK, T)):
                     nc.tensor.matmul_mx(
                         out=acc[:, 0 : hi - lo],
@@ -116,70 +122,78 @@ def tile_moe_sup_lin_relu_kernel(
                         start=(g == 0),
                         stop=(g == PASSES - 1),
                     )
-        h_pairs = [held("h_pairs%d" % u, [P, T, PAIR], BF16) for u in range(2)]
+        h_pairs = [held("h_pairs%d" % u, [P, WINDOW, PAIR], BF16) for u in range(2)]
+        for u in range(2):
+            nc.gpsimd.memset(h_pairs[u][:, T:WINDOW, :].rearrange("p t e -> p (t e)").bitcast(I32), 0)
         for t in range(PACK):
             for acc, lo, hi in ((wide[t], 0, BANK), (rest[t], BANK, T)):
                 dst = h_pairs[t // PAIR][:, lo:hi, t % PAIR]
-                if t < PAIR:
+                if t >= PAIR:
                     nc.scalar.activation(out=dst, in_=acc[:, 0 : hi - lo], func=RELU)
                 else:
                     nc.vector.tensor_scalar_max(out=dst, in0=acc[:, 0 : hi - lo], scalar1=0.0)
 
-        h_codes = [held("h_codes%d" % d, [P, 2 * C], U32) for d in range(E // 2)]
-        h_scales = [held("h_scales%d" % d, [P, 2 * C], U8) for d in range(E // 2)]
+        h_codes = [held("h_codes%d" % first, [P, count * C], U32) for first, count in EXPERT_RUNS]
+        h_scales = [held("h_scales%d" % first, [P, count * C], U8) for first, count in EXPERT_RUNS]
 
-        def gather_duo(d):
-            picked = ringed("picked", [P, 2, 2 * C], U32, 2)
+        def gather_run(d):
+            first, count = EXPERT_RUNS[d]
+            picked = ringed("picked", [P, 2, count * C], U32, 2)
             for u in range(2):
                 window = h_pairs[u][:].rearrange("p t e -> p (t e)").bitcast(U32)
-                nc.vector.tensor_copy(out=picked[:, u, :], in_=window.indirect(slot_tokens[:, 16 * d : 16 * (d + 1)]))
+                offsets = slot_tokens[:, first * C // 16 : (first + count) * C // 16]
+                nc.vector.tensor_copy(out=picked[:, u, :], in_=window.indirect(offsets))
             return picked
 
-        def weave_duo(picked):
-            woven = ringed("woven", [P, 2 * C * PACK], BF16, 2)
+        def weave_run(d, picked):
+            woven = ringed("woven", [P, EXPERT_RUNS[d][1] * C * PACK], BF16, 2)
             nc.vector.tensor_copy(
                 out=woven[:].bitcast(I32).rearrange("p (s u) -> p s u", u=2),
                 in_=picked[:].bitcast(I32).rearrange("p u s -> p s u"),
             )
             return woven
 
-        def quantise_duo(d, woven):
+        def quantise_run(d, woven):
             nc.vector.quantize_mx(out=h_codes[d][:].bitcast(FP8X4), scales=h_scales[d][:], in_=woven[:])
 
-        def round_piece(half, e):
-            if half == 1 and e in BEHIND.values():
-                grouped = held("behind%d" % e, [P, PIECE * PACK], BF16)
+        def w2_duo(half, first):
+            if (half, first) in ((0, 8), (1, 0)):
+                grouped = held("turn_of_halves", [P, 2, PIECE * PACK], BF16)
+            elif (half, first) == (1, 8):
+                grouped = held("last_duo", [P, 2, PIECE * PACK], BF16)
             else:
-                grouped = ringed("w2_grouped", [P, PIECE * PACK], BF16, 11)
-            copy = nc.vector.tensor_copy if (half, e) in ON_VECTOR else nc.scalar.copy
-            copy(
-                out=grouped[:].rearrange("p (c i j) -> p c j i", i=4, j=PACK),
-                in_=w2_raw[half, e][:].rearrange("p j (c i) -> p c j i", i=4),
+                grouped = ringed("w2_grouped", [P, 2, PIECE * PACK], BF16, 5)
+            for e in (first, first + 1):
+                copy = nc.vector.tensor_copy if (half, e) in ON_VECTOR else nc.scalar.copy
+                copy(
+                    out=grouped[:, e % 2, :].rearrange("p (c i j) -> p c j i", i=4, j=PACK),
+                    in_=w2_raw[half, e][:].rearrange("p j (c i) -> p c j i", i=4),
+                )
+            codes = ringed("w2_codes", [P, 2 * PIECE], U32, 6)
+            scales = ringed("w2_scales", [P, 2 * PIECE], U8, 6)
+            nc.vector.quantize_mx(
+                out=codes[:].bitcast(FP8X4), scales=scales[:], in_=grouped[:].rearrange("p e c -> p (e c)")
             )
-            return grouped
-
-        def quantise_piece(grouped):
-            codes = ringed("w2_codes", [P, PIECE], U32, 12)
-            scales = ringed("w2_scales", [P, PIECE], U8, 12)
-            nc.vector.quantize_mx(out=codes[:].bitcast(FP8X4), scales=scales[:], in_=grouped[:])
             return codes, scales
 
         y = [held("y%d" % c, [P, SLOTS], F32) for c in range(N // P)]
         turn = [0]
 
-        def expert_run(half, first, count, pieces):
+        def expert_run(half, d, duos):
+            first, count = EXPERT_RUNS[d]
             for b in range(BLOCKS):
                 acc = bank(turn[0] % 4)
                 turn[0] = turn[0] + 1
                 for e in range(first, first + count):
-                    codes, scales = pieces[e]
-                    cols = slice((e % 2) * C, (e % 2 + 1) * C)
+                    codes, scales = duos[e // 2]
+                    cols = slice((e - first) * C, (e - first + 1) * C)
+                    rows = slice((e % 2) * PIECE + b * P, (e % 2) * PIECE + (b + 1) * P)
                     nc.tensor.matmul_mx(
-                        out=acc[:, (e - first) * C : (e - first + 1) * C],
-                        lhsT=codes[:, b * P : (b + 1) * P].bitcast(FP8X4),
-                        lhsT_scale=scales[:, b * P : (b + 1) * P],
-                        rhs=h_codes[e // 2][:, cols].bitcast(FP8X4),
-                        rhs_scale=h_scales[e // 2][:, cols],
+                        out=acc[:, cols],
+                        lhsT=codes[:, rows].bitcast(FP8X4),
+                        lhsT_scale=scales[:, rows],
+                        rhs=h_codes[d][:, cols].bitcast(FP8X4),
+                        rhs_scale=h_scales[d][:, cols],
                         start=True,
                         stop=True,
                     )
@@ -190,23 +204,20 @@ def tile_moe_sup_lin_relu_kernel(
         out_codes = held("out_codes", [P, T], U32)
         out_scales = held("out_scales", [P, T], U8)
 
-        def combine(half, i):
-            lo, n = TOKEN_CHUNKS[i]
-            terms = []
+        def combine(half, lo, n):
+            if half == 0 and lo > 0:
+                terms = held("last_duo", [P, 2, BLOCKS, n], F32)
+            else:
+                terms = ringed("terms", [P, 2, BLOCKS, n], F32, 2)
             for r in range(2):
-                if half == 0 and i in BEHIND:
-                    term = held("behind%d" % BEHIND[i], [P, BLOCKS, n], F32) if r == 0 else held("second%d" % i, [P, BLOCKS, n], F32)
-                else:
-                    term = ringed("term%d" % r, [P, BLOCKS, n], F32, 2)
                 for b in range(BLOCKS):
                     nc.vector.tensor_tensor(
-                        term[:, b, :],
+                        terms[:, r, b, :],
                         y[half * BLOCKS + b][:].indirect(token_slots[r][:, lo // 16 : (lo + n) // 16]),
                         gates[:, r, lo : lo + n],
                         MULT,
                     )
-                terms.append(term)
-            nc.vector.tensor_tensor(result[half][:, :, lo : lo + n], terms[0][:], terms[1][:], ADD)
+            nc.vector.tensor_tensor(result[half][:, :, lo : lo + n], terms[:, 0], terms[:, 1], ADD)
 
         def store_result(half, lo, n):
             rows = out_0[half * PIECE : (half + 1) * PIECE, lo : lo + n]
@@ -243,37 +254,31 @@ def tile_moe_sup_lin_relu_kernel(
                 in_=out_codes[:, lo : lo + n].bitcast(I32),
             )
 
-        pieces = {}
-        picked = gather_duo(0)
-        for d in range(E // 2):
-            grouped = [round_piece(0, e) for e in (2 * d, 2 * d + 1)]
-            woven = weave_duo(picked)
-            if d + 1 < E // 2:
-                picked = gather_duo(d + 1)
-            quantise_duo(d, woven)
-            for e in (2 * d, 2 * d + 1):
-                pieces[e] = quantise_piece(grouped[e % 2])
-            for first, count in EXPERT_RUNS:
-                if first + count == 2 * d + 2:
-                    expert_run(0, first, count, pieces)
+        duos = []
+        picked = gather_run(0)
+        for d, (first, count) in enumerate(EXPERT_RUNS):
+            woven = weave_run(d, picked)
+            if d + 1 < len(EXPERT_RUNS):
+                picked = gather_run(d + 1)
+            quantise_run(d, woven)
+            for e in range(first, first + count, 2):
+                duos.append(w2_duo(0, e))
+            expert_run(0, d, duos)
 
-        pieces = {}
-        for e in range(E):
-            pieces[e] = quantise_piece(round_piece(1, e))
-            for first, count in EXPERT_RUNS:
-                if first + count == e + 1:
-                    expert_run(1, first, count, pieces)
-            if e == 0:
-                combine(0, 0)
-            for i in BEHIND:
-                if BEHIND[i] == e:
-                    combine(0, i)
+        duos = []
+        for d, (first, count) in enumerate(EXPERT_RUNS):
+            for e in range(first, first + count, 2):
+                duos.append(w2_duo(1, e))
+                if e == 0:
+                    combine(0, *EARLY_CHUNKS[0])
+            expert_run(1, d, duos)
+        combine(0, *EARLY_CHUNKS[1])
         store_result(0, 0, T)
         for i in range(len(TOKEN_CHUNKS)):
             turn_to_tokens(0, i)
 
         for i, (lo, n) in enumerate(TOKEN_CHUNKS):
-            combine(1, i)
+            combine(1, lo, n)
             store_result(1, lo, n)
             turn_to_tokens(1, i)
             turn_back(i)

@@ -28,10 +28,12 @@ PAIR = 2
 BANK = 512
 TOKEN_CHUNKS = [(0, 256), (256, 256), (512, 128)]
 EXPERT_RUNS = [(0, 4), (4, 4), (8, 2)]
-ON_VECTOR = {(1, 0), (1, 1), (1, 9)}
+ON_VECTOR = {(1, 0), (1, 1), (1, 2), (1, 3)}
+WHOLE = 4
+W1_SPLIT = 84
 EARLY_CHUNKS = [(0, 512), (512, 128)]
 WINDOW = 704
-Y_AFTER = {(0, 9): "y0", (0, 8): "y1", (1, 8): "y2", (1, 7): "y3"}
+Y_AFTER = {(0, 9): "y0", (0, 8): "y1", (1, 9): "y2", (1, 8): "y3"}
 
 
 def tile_moe_sup_lin_relu_kernel(
@@ -52,13 +54,19 @@ def tile_moe_sup_lin_relu_kernel(
         def ringed(name, shape, dtype, bufs):
             return ring.tile(shape, dtype, name=name, bufs=bufs, align_bytes=64)
 
-        def load_piece(rows, name=None):
-            if name is None:
-                raw = ringed("raw", [P, PACK, PIECE], F32, 16)
-            else:
-                raw = held(name, [P, PACK, PIECE], F32)
+        def load_rows(raw, rows):
             nc.sync.dma_start(out=raw[:], in_=rows.rearrange("(p j) c -> p j c", j=PACK))
             return raw
+
+        def load_whole(rows):
+            return load_rows(ringed("raw_whole", [P, PACK, N], F32, 5), rows)
+
+        def load_half(half, e):
+            if (half, e) in Y_AFTER:
+                raw = held(Y_AFTER[half, e], [P, PACK, PIECE], F32)
+            else:
+                raw = ringed("raw_half", [P, PACK, PIECE], F32, 6)
+            return load_rows(raw, w2[e, :, half * PIECE : (half + 1) * PIECE])[:]
 
         x_planes = held("x_planes", [P, T], U8)
         nc.vector.memset(x_planes[:].bitcast(I32), 0)
@@ -67,19 +75,21 @@ def tile_moe_sup_lin_relu_kernel(
                 out=x_planes[32 * q : 32 * q + 16, :].bitcast(I32),
                 in_=x_scales[:, 4 * q : 4 * q + 4, :].bitcast(I32),
             )
-        w1_raw, x_codes = {}, []
+        w1_raw, x_codes = [], []
         for g in range(PASSES):
-            for s in range(2):
-                w1_raw[g, s] = load_piece(w1[g * 512 : (g + 1) * 512, s * PIECE : (s + 1) * PIECE])
-            for gx in (g,):
-                words = held("x_codes%d" % gx, [P, T], U32)
-                nc.sync.dma_start(out=words[:].bitcast(I32), in_=x_words[gx].rearrange("p t d -> p (t d)").bitcast(I32))
-                x_codes.append(words)
+            w1_raw.append(load_whole(w1[g * 512 : (g + 1) * 512, :]))
+            words = held("x_codes%d" % g, [P, T], U32)
+            nc.sync.dma_start(out=words[:].bitcast(I32), in_=x_words[g].rearrange("p t d -> p (t d)").bitcast(I32))
+            x_codes.append(words)
         slot_tokens = held("slot_tokens", [P, SLOTS // 16], U16)
         nc.sync.dma_start(slot_tokens[:], offs)
         w2_raw = {}
-        for e in range(E):
-            w2_raw[0, e] = load_piece(w2[e, :, 0:PIECE], Y_AFTER.get((0, e)))
+        for e in range(WHOLE):
+            raw = load_whole(w2[e])
+            for half in range(HALVES):
+                w2_raw[half, e] = raw[:, :, half * PIECE : (half + 1) * PIECE]
+        for e in range(WHOLE, E):
+            w2_raw[0, e] = load_half(0, e)
         token_slots = []
         for r, pos in enumerate((pos1, pos2)):
             lst = held("token_slots%d" % r, [P, T // 16], U16)
@@ -87,8 +97,8 @@ def tile_moe_sup_lin_relu_kernel(
             token_slots.append(lst)
         gates = held("gates", [P, 2, T], F32)
         nc.sync.dma_start(out=gates[:], in_=gate.rearrange("r p t -> p r t"))
-        for e in range(E):
-            w2_raw[1, e] = load_piece(w2[e, :, PIECE : 2 * PIECE], Y_AFTER.get((1, e)))
+        for e in range(WHOLE, E):
+            w2_raw[1, e] = load_half(1, e)
 
         ident = held("ident", [P, P], F32)
         make_identity(nc, ident[:])
@@ -97,10 +107,10 @@ def tile_moe_sup_lin_relu_kernel(
         rest = [bank(PACK + t) for t in range(PACK)]
         for g in range(PASSES):
             dealt = ringed("w1_dealt", [P, PACK, P, PACK], BF16, 2)
-            for s, copy in enumerate((nc.scalar.copy, nc.vector.tensor_copy)):
+            for copy, lo, hi in ((nc.vector.tensor_copy, 0, W1_SPLIT), (nc.scalar.copy, W1_SPLIT, P)):
                 copy(
-                    out=dealt[:, :, 64 * s : 64 * (s + 1), :].rearrange("p t m j -> p m j t"),
-                    in_=w1_raw[g, s][:].rearrange("p j (m t) -> p m j t", t=PACK),
+                    out=dealt[:, :, lo:hi, :].rearrange("p t m j -> p m j t"),
+                    in_=w1_raw[g][:, :, PACK * lo : PACK * hi].rearrange("p j (m t) -> p m j t", t=PACK),
                 )
             codes = ringed("w1_codes", [P, H], U32, 2)
             scales = ringed("w1_scales", [P, H], U8, 2)
@@ -157,7 +167,7 @@ def tile_moe_sup_lin_relu_kernel(
             nc.vector.quantize_mx(out=h_codes[d][:].bitcast(FP8X4), scales=h_scales[d][:], in_=woven[:])
 
         def w2_duo(half, first):
-            if (half, first) in ((0, 8), (1, 0)):
+            if (half, first) in ((0, 8), (1, 2)):
                 grouped = held("turn_of_halves", [P, 2, PIECE * PACK], BF16)
             elif (half, first) == (1, 8):
                 grouped = held("last_duo", [P, 2, PIECE * PACK], BF16)
@@ -167,7 +177,7 @@ def tile_moe_sup_lin_relu_kernel(
                 copy = nc.vector.tensor_copy if (half, e) in ON_VECTOR else nc.scalar.copy
                 copy(
                     out=grouped[:, e % 2, :].rearrange("p (c i j) -> p c j i", i=4, j=PACK),
-                    in_=w2_raw[half, e][:].rearrange("p j (c i) -> p c j i", i=4),
+                    in_=w2_raw[half, e].rearrange("p j (c i) -> p c j i", i=4),
                 )
             codes = ringed("w2_codes", [P, 2 * PIECE], U32, 6)
             scales = ringed("w2_scales", [P, 2 * PIECE], U8, 6)
@@ -269,7 +279,7 @@ def tile_moe_sup_lin_relu_kernel(
         for d, (first, count) in enumerate(EXPERT_RUNS):
             for e in range(first, first + count, 2):
                 duos.append(w2_duo(1, e))
-                if e == 0:
+                if e == 2:
                     combine(0, *EARLY_CHUNKS[0])
             expert_run(1, d, duos)
         combine(0, *EARLY_CHUNKS[1])

@@ -68,6 +68,11 @@ def tile_moe_sup_lin_relu_kernel(
                 raw = ringed("raw_half", [P, PACK, PIECE], F32, 6)
             return load_rows(raw, w2[e, :, half * PIECE : (half + 1) * PIECE])[:]
 
+        gate_wide = held("gate_wide", [P, 2, PACK], F32)
+        nc.sync.dma_start(out=gate_wide[:], in_=gate[:, 0, 0:BANK].rearrange("r (p c) -> p r c", c=PACK))
+        gate_rest = held("gate_rest", [P, 2], F32)
+        with nc.allow_non_contiguous_dma(reason="one gate value a partition"):
+            nc.sync.dma_start(out=gate_rest[:], in_=gate[:, 0, BANK:T].rearrange("r p -> p r"))
         x_planes = held("x_planes", [P, T], U8)
         nc.vector.memset(x_planes[:].bitcast(I32), 0)
         for q in range(4):
@@ -95,13 +100,25 @@ def tile_moe_sup_lin_relu_kernel(
             lst = held("token_slots%d" % r, [P, T // 16], U16)
             nc.sync.dma_start(lst[:], pos)
             token_slots.append(lst)
-        gates = held("gates", [P, 2, T], F32)
-        nc.sync.dma_start(out=gates[:], in_=gate.rearrange("r p t -> p r t"))
         for e in range(WHOLE, E):
             w2_raw[1, e] = load_half(1, e)
 
         ident = held("ident", [P, P], F32)
         make_identity(nc, ident[:])
+
+        gates = held("gates", [P, 2, T], F32)
+        for r in range(2):
+            acc = bank(5 + r)
+            for c in range(PACK):
+                nc.tensor.transpose(acc[:, c * P : (c + 1) * P], gate_wide[:, r, c : c + 1].to_broadcast([P, P]), ident[:])
+            nc.scalar.copy(
+                out=gates[:, r, 0:BANK].rearrange("j (p c) -> j p c", c=PACK),
+                in_=acc[:].rearrange("j (c p) -> j p c", c=PACK),
+            )
+        acc = bank(7)
+        for r in range(2):
+            nc.tensor.transpose(acc[:, r * P : (r + 1) * P], gate_rest[:, r : r + 1].to_broadcast([P, P]), ident[:])
+        nc.scalar.copy(out=gates[:, :, BANK:T], in_=acc[:, 0 : 2 * P].rearrange("j (r p) -> j r p", r=2))
 
         wide = [bank(t) for t in range(PACK)]
         rest = [bank(PACK + t) for t in range(PACK)]
@@ -209,16 +226,12 @@ def tile_moe_sup_lin_relu_kernel(
                     )
                 nc.scalar.copy(out=y[half * BLOCKS + b][:, first * C : (first + count) * C], in_=acc[:, 0 : count * C])
 
-        result = [held("result%d" % half, [P, BLOCKS, T], F32) for half in range(HALVES)]
         by_token = [held("by_token%d" % i, [P, n // P, 2, P, PAIR], BF16) for i, (lo, n) in enumerate(TOKEN_CHUNKS)]
         out_codes = held("out_codes", [P, T], U32)
         out_scales = held("out_scales", [P, T], U8)
+        token_terms = {}
 
-        def combine(half, lo, n):
-            if half == 0 and lo > 0:
-                terms = held("last_duo", [P, 2, BLOCKS, n], F32)
-            else:
-                terms = ringed("terms", [P, 2, BLOCKS, n], F32, 2)
+        def gated_terms(terms, half, lo, n):
             for r in range(2):
                 for b in range(BLOCKS):
                     nc.vector.tensor_tensor(
@@ -227,19 +240,28 @@ def tile_moe_sup_lin_relu_kernel(
                         gates[:, r, lo : lo + n],
                         MULT,
                     )
-            nc.vector.tensor_tensor(result[half][:, :, lo : lo + n], terms[:, 0], terms[:, 1], ADD)
+            for at in range(0, n, P):
+                token_terms[half, lo + at] = terms[:, :, :, at : at + P]
+            return terms
 
-        def store_result(half, lo, n):
+        def add_terms(result, terms):
+            nc.vector.tensor_tensor(result, terms[:, 0], terms[:, 1], ADD)
+
+        def store_result(result, half, lo, n):
             rows = out_0[half * PIECE : (half + 1) * PIECE, lo : lo + n]
-            nc.sync.dma_start(out=rows.rearrange("(b q) t -> q b t", q=P), in_=result[half][:, :, lo : lo + n])
+            nc.sync.dma_start(out=rows.rearrange("(b q) t -> q b t", q=P), in_=result)
 
         def turn_to_tokens(half, i):
             lo, n = TOKEN_CHUNKS[i]
             acc = bank(2 + 2 * half + i % 2)
             for kk in range(n // P):
+                terms = token_terms[half, lo + kk * P]
                 for b in range(BLOCKS):
                     at = (kk * BLOCKS + b) * P
-                    nc.tensor.transpose(acc[:, at : at + P], result[half][:, b, lo + kk * P : lo + (kk + 1) * P], ident[:])
+                    for r in range(2):
+                        nc.tensor.matmul(
+                            acc[:, at : at + P], terms[:, r, b, :], ident[:], is_transpose=True, start=(r == 0), stop=(r == 1)
+                        )
             nc.scalar.copy(
                 out=by_token[i][:, :, :, 64 * half : 64 * (half + 1), :],
                 in_=acc[:, 0 : n * BLOCKS].rearrange("k (kk p u e) -> k kk u p e", p=64, u=2, e=PAIR),
@@ -280,18 +302,26 @@ def tile_moe_sup_lin_relu_kernel(
             for e in range(first, first + count, 2):
                 duos.append(w2_duo(1, e))
                 if e == 2:
-                    combine(0, *EARLY_CHUNKS[0])
+                    early = [gated_terms(held("early_terms", [P, 2, BLOCKS, EARLY_CHUNKS[0][1]], F32), 0, *EARLY_CHUNKS[0])]
             expert_run(1, d, duos)
-        combine(0, *EARLY_CHUNKS[1])
-        store_result(0, 0, T)
+        early.append(gated_terms(held("last_duo", [P, 2, BLOCKS, EARLY_CHUNKS[1][1]], F32), 0, *EARLY_CHUNKS[1]))
+        result = held("early_result", [P, BLOCKS, EARLY_CHUNKS[1][1]], F32)
+        add_terms(result[:], early[1])
+        store_result(result[:], 0, *EARLY_CHUNKS[1])
         for i in range(len(TOKEN_CHUNKS)):
             turn_to_tokens(0, i)
 
         for i, (lo, n) in enumerate(TOKEN_CHUNKS):
-            combine(1, lo, n)
-            store_result(1, lo, n)
+            terms = gated_terms(ringed("terms", [P, 2, BLOCKS, n], F32, 2), 1, lo, n)
             turn_to_tokens(1, i)
+            result = held("result%d" % i, [P, BLOCKS, n], F32)
+            add_terms(result[:], terms)
+            store_result(result[:], 1, lo, n)
             turn_back(i)
+        result = held("y3", [P, BLOCKS, EARLY_CHUNKS[0][1]], F32)
+        for lo, n in TOKEN_CHUNKS[:2]:
+            add_terms(result[:, :, lo : lo + n], early[0][:, :, :, lo : lo + n])
+            store_result(result[:, :, lo : lo + n], 0, lo, n)
         for q in range(4):
             queue = nc.sync if q % 2 == 0 else nc.scalar
             queue.dma_start(

@@ -28,12 +28,12 @@ PAIR = 2
 BANK = 512
 TOKEN_CHUNKS = [(0, 256), (256, 256), (512, 128)]
 EXPERT_RUNS = [(0, 4), (4, 4), (8, 2)]
-ON_VECTOR = {(1, 0), (1, 1), (1, 2), (1, 3)}
+ON_VECTOR = {(0, 9), (1, 1), (1, 2), (1, 3), (1, 9)}
 WHOLE = 4
 W1_SPLIT = 84
 EARLY_CHUNKS = [(0, 512), (512, 128)]
 WINDOW = 704
-Y_AFTER = {(0, 9): "y0", (0, 8): "y1", (1, 9): "y2", (1, 8): "y3"}
+Y_AFTER = {(0, 8): "y0", (0, 7): "y1", (1, 8): "y2", (1, 7): "y3"}
 
 
 def tile_moe_sup_lin_relu_kernel(
@@ -196,8 +196,8 @@ def tile_moe_sup_lin_relu_kernel(
                     out=grouped[:, e % 2, :].rearrange("p (c i j) -> p c j i", i=4, j=PACK),
                     in_=w2_raw[half, e].rearrange("p j (c i) -> p c j i", i=4),
                 )
-            codes = ringed("w2_codes", [P, 2 * PIECE], U32, 6)
-            scales = ringed("w2_scales", [P, 2 * PIECE], U8, 6)
+            codes = ringed("w2_codes", [P, 2 * PIECE], U32, 8)
+            scales = ringed("w2_scales", [P, 2 * PIECE], U8, 8)
             nc.vector.quantize_mx(
                 out=codes[:].bitcast(FP8X4), scales=scales[:], in_=grouped[:].rearrange("p e c -> p (e c)")
             )
@@ -295,11 +295,13 @@ def tile_moe_sup_lin_relu_kernel(
             quantise_run(d, woven)
             for e in range(first, first + count, 2):
                 duos.append(w2_duo(0, e))
+                if e == 0:
+                    early_duo = w2_duo(1, 0)
             expert_run(0, d, duos)
 
-        duos = []
+        duos = [early_duo]
         for d, (first, count) in enumerate(EXPERT_RUNS):
-            for e in range(first, first + count, 2):
+            for e in range(max(first, 2), first + count, 2):
                 duos.append(w2_duo(1, e))
                 if e == 2:
                     early = [gated_terms(held("early_terms", [P, 2, BLOCKS, EARLY_CHUNKS[0][1]], F32), 0, *EARLY_CHUNKS[0])]

from contextlib import ExitStack

import concourse.mybir as mybir
from concourse.masks import make_identity

K, T, E, C, H, N = 2048, 640, 10, 128, 512, 512
SLOTS = E * C
FLOPS = 2 * K * H * T + 2 * H * N * SLOTS

F32 = mybir.dt.float32
BF16 = mybir.dt.bfloat16
I32 = mybir.dt.int32
U32 = mybir.dt.uint32
U16 = mybir.dt.uint16
U8 = mybir.dt.uint8
FP8X4 = mybir.dt.float8_e4m3fn_x4
MULT = mybir.AluOpType.mult
ADD = mybir.AluOpType.add
RELU = mybir.ActivationFunctionType.Relu

P = 128
PACK = 4
PASSES = K // (P * PACK)
PIECE = 256
HALVES = N // PIECE
BLOCKS = PIECE // P
PAIR = 2
BANK = 512
TOKEN_CHUNKS = [(0, 256), (256, 256), (512, 128)]
EXPERT_RUNS = [(0, 4), (4, 4), (8, 2)]
ON_VECTOR = {(0, 9), (1, 1), (1, 2), (1, 3), (1, 9)}
WHOLE = 4
W1_SPLIT = 84
EARLY_CHUNKS = [(0, 512), (512, 128)]
WINDOW = 704
Y_AFTER = {(0, 8): "y0", (0, 7): "y1", (1, 8): "y2", (1, 7): "y3"}


def tile_moe_sup_lin_relu_kernel(
    tc, x_words, x_scales, w1, w2, gate, offs, pos1, pos2, out_0, out_1, out_2
):
    nc = tc.nc
    with ExitStack() as ctx:
        keep = ctx.enter_context(tc.tile_pool(name="keep", bufs=1))
        ring = ctx.enter_context(tc.tile_pool(name="ring", bufs=2))
        psum = ctx.enter_context(tc.psum_pool(name="psum", bufs=1))

        def bank(b):
            return psum.tile([P, BANK], F32, name="bank%d" % b)

        def held(name, shape, dtype):
            return keep.tile(shape, dtype, name=name, align_bytes=64)

        def ringed(name, shape, dtype, bufs):
            return ring.tile(shape, dtype, name=name, bufs=bufs, align_bytes=64)

        def load_rows(raw, rows):
            nc.sync.dma_start(out=raw[:], in_=rows.rearrange("(p j) c -> p j c", j=PACK))
            return raw

        def load_whole(rows):
            return load_rows(ringed("raw_whole", [P, PACK, N], F32, 5), rows)

        def load_half(half, e):
            if (half, e) in Y_AFTER:
                raw = held(Y_AFTER[half, e], [P, PACK, PIECE], F32)
            else:
                raw = ringed("raw_half", [P, PACK, PIECE], F32, 6)
            return load_rows(raw, w2[e, :, half * PIECE : (half + 1) * PIECE])[:]

        gate_wide = held("gate_wide", [P, 2, PACK], F32)
        nc.sync.dma_start(out=gate_wide[:], in_=gate[:, 0, 0:BANK].rearrange("r (p c) -> p r c", c=PACK))
        gate_rest = held("gate_rest", [P, 2], F32)
        with nc.allow_non_contiguous_dma(reason="one gate value a partition"):
            nc.sync.dma_start(out=gate_rest[:], in_=gate[:, 0, BANK:T].rearrange("r p -> p r"))
        x_planes = held("x_planes", [P, T], U8)
        nc.vector.memset(x_planes[:].bitcast(I32), 0)
        for q in range(4):
            nc.scalar.dma_start(
                out=x_planes[32 * q : 32 * q + 16, :].bitcast(I32),
                in_=x_scales[:, 4 * q : 4 * q + 4, :].bitcast(I32),
            )
        w1_raw, x_codes = [], []
        for g in range(PASSES):
            w1_raw.append(load_whole(w1[g * 512 : (g + 1) * 512, :]))
            words = held("x_codes%d" % g, [P, T], U32)
            nc.sync.dma_start(out=words[:].bitcast(I32), in_=x_words[g].rearrange("p t d -> p (t d)").bitcast(I32))
            x_codes.append(words)
        slot_tokens = held("slot_tokens", [P, SLOTS // 16], U16)
        nc.sync.dma_start(slot_tokens[:], offs)
        w2_raw = {}
        for e in range(WHOLE):
            raw = load_whole(w2[e])
            for half in range(HALVES):
                w2_raw[half, e] = raw[:, :, half * PIECE : (half + 1) * PIECE]
        for e in range(WHOLE, E):
            w2_raw[0, e] = load_half(0, e)
        token_slots = []
        for r, pos in enumerate((pos1, pos2)):
            lst = held("token_slots%d" % r, [P, T // 16], U16)
            nc.sync.dma_start(lst[:], pos)
            token_slots.append(lst)
        for e in range(WHOLE, E):
            w2_raw[1, e] = load_half(1, e)

        ident = held("ident", [P, P], F32)
        make_identity(nc, ident[:])

        gates = held("gates", [P, 2, T], F32)
        for r in range(2):
            acc = bank(5 + r)
            for c in range(PACK):
                nc.tensor.transpose(acc[:, c * P : (c + 1) * P], gate_wide[:, r, c : c + 1].to_broadcast([P, P]), ident[:])
            nc.scalar.copy(
                out=gates[:, r, 0:BANK].rearrange("j (p c) -> j p c", c=PACK),
                in_=acc[:].rearrange("j (c p) -> j p c", c=PACK),
            )
        acc = bank(7)
        for r in range(2):
            nc.tensor.transpose(acc[:, r * P : (r + 1) * P], gate_rest[:, r : r + 1].to_broadcast([P, P]), ident[:])
        nc.scalar.copy(out=gates[:, :, BANK:T], in_=acc[:, 0 : 2 * P].rearrange("j (r p) -> j r p", r=2))

        wide = [bank(t) for t in range(PACK)]
        rest = [bank(PACK + t) for t in range(PACK)]
        for g in range(PASSES):
            dealt = ringed("w1_dealt", [P, PACK, P, PACK], BF16, 2)
            for copy, lo, hi in ((nc.vector.tensor_copy, 0, W1_SPLIT), (nc.scalar.copy, W1_SPLIT, P)):
                copy(
                    out=dealt[:, :, lo:hi, :].rearrange("p t m j -> p m j t"),
                    in_=w1_raw[g][:, :, PACK * lo : PACK * hi].rearrange("p j (m t) -> p m j t", t=PACK),
                )
            codes = ringed("w1_codes", [P, H], U32, 2)
            scales = ringed("w1_scales", [P, H], U8, 2)
            for u in range(2):
                cols = slice(u * PAIR * P, (u + 1) * PAIR * P)
                nc.vector.quantize_mx(
                    out=codes[:, cols].bitcast(FP8X4),
                    scales=scales[:, cols],
                    in_=dealt[:, PAIR * u : PAIR * (u + 1)].rearrange("p t m j -> p (t m j)"),
                )
            for t in range(PACK):
                for acc, lo, hi in ((wide[t], 0, BANK), (rest[t], BANK, T)):
                    nc.tensor.matmul_mx(
                        out=acc[:, 0 : hi - lo],
                        lhsT=codes[:, t * P : (t + 1) * P].bitcast(FP8X4),
                        lhsT_scale=scales[:, t * P : (t + 1) * P],
                        rhs=x_codes[g][:, lo:hi].bitcast(FP8X4),
                        rhs_scale=x_planes[4 * g : P, lo:hi],
                        start=(g == 0),
                        stop=(g == PASSES - 1),
                    )
        h_pairs = [held("h_pairs%d" % u, [P, WINDOW, PAIR], BF16) for u in range(2)]
        for u in range(2):
            nc.gpsimd.memset(h_pairs[u][:, T:WINDOW, :].rearrange("p t e -> p (t e)").bitcast(I32), 0)
        for t in range(PACK):
            for acc, lo, hi in ((wide[t], 0, BANK), (rest[t], BANK, T)):
                dst = h_pairs[t // PAIR][:, lo:hi, t % PAIR]
                if t >= PAIR:
                    nc.scalar.activation(out=dst, in_=acc[:, 0 : hi - lo], func=RELU)
                else:
                    nc.vector.tensor_scalar_max(out=dst, in0=acc[:, 0 : hi - lo], scalar1=0.0)

        h_codes = [held("h_codes%d" % first, [P, count * C], U32) for first, count in EXPERT_RUNS]
        h_scales = [held("h_scales%d" % first, [P, count * C], U8) for first, count in EXPERT_RUNS]

        def gather_run(d):
            first, count = EXPERT_RUNS[d]
            picked = ringed("picked", [P, 2, count * C], U32, 2)
            for u in range(2):
                window = h_pairs[u][:].rearrange("p t e -> p (t e)").bitcast(U32)
                offsets = slot_tokens[:, first * C // 16 : (first + count) * C // 16]
                nc.vector.tensor_copy(out=picked[:, u, :], in_=window.indirect(offsets))
            return picked

        def weave_run(d, picked):
            woven = ringed("woven", [P, EXPERT_RUNS[d][1] * C * PACK], BF16, 2)
            nc.vector.tensor_copy(
                out=woven[:].bitcast(I32).rearrange("p (s u) -> p s u", u=2),
                in_=picked[:].bitcast(I32).rearrange("p u s -> p s u"),
            )
            return woven

        def quantise_run(d, woven):
            nc.vector.quantize_mx(out=h_codes[d][:].bitcast(FP8X4), scales=h_scales[d][:], in_=woven[:])

        def w2_duo(half, first):
            if (half, first) in ((0, 8), (1, 2)):
                grouped = held("turn_of_halves", [P, 2, PIECE * PACK], BF16)
            elif (half, first) == (1, 8):
                grouped = held("last_duo", [P, 2, PIECE * PACK], BF16)
            else:
                grouped = ringed("w2_grouped", [P, 2, PIECE * PACK], BF16, 5)
            for e in (first, first + 1):
                copy = nc.vector.tensor_copy if (half, e) in ON_VECTOR else nc.scalar.copy
                copy(
                    out=grouped[:, e % 2, :].rearrange("p (c i j) -> p c j i", i=4, j=PACK),
                    in_=w2_raw[half, e].rearrange("p j (c i) -> p c j i", i=4),
                )
            codes = ringed("w2_codes", [P, 2 * PIECE], U32, 8)
            scales = ringed("w2_scales", [P, 2 * PIECE], U8, 8)
            nc.vector.quantize_mx(
                out=codes[:].bitcast(FP8X4), scales=scales[:], in_=grouped[:].rearrange("p e c -> p (e c)")
            )
            return codes, scales

        y = [held("y%d" % c, [P, SLOTS], F32) for c in range(N // P)]
        turn = [0]

        def expert_run(half, d, duos):
            first, count = EXPERT_RUNS[d]
            for b in range(BLOCKS):
                acc = bank(turn[0] % 4)
                turn[0] = turn[0] + 1
                for e in range(first, first + count):
                    codes, scales = duos[e // 2]
                    cols = slice((e - first) * C, (e - first + 1) * C)
                    rows = slice((e % 2) * PIECE + b * P, (e % 2) * PIECE + (b + 1) * P)
                    nc.tensor.matmul_mx(
                        out=acc[:, cols],
                        lhsT=codes[:, rows].bitcast(FP8X4),
                        lhsT_scale=scales[:, rows],
                        rhs=h_codes[d][:, cols].bitcast(FP8X4),
                        rhs_scale=h_scales[d][:, cols],
                        start=True,
                        stop=True,
                    )
                nc.scalar.copy(out=y[half * BLOCKS + b][:, first * C : (first + count) * C], in_=acc[:, 0 : count * C])

        by_token = [held("by_token%d" % i, [P, n // P, 2, P, PAIR], BF16) for i, (lo, n) in enumerate(TOKEN_CHUNKS)]
        out_codes = held("out_codes", [P, T], U32)
        out_scales = held("out_scales", [P, T], U8)
        token_terms = {}

        def gated_terms(terms, half, lo, n):
            for r in range(2):
                for b in range(BLOCKS):
                    nc.vector.tensor_tensor(
                        terms[:, r, b, :],
                        y[half * BLOCKS + b][:].indirect(token_slots[r][:, lo // 16 : (lo + n) // 16]),
                        gates[:, r, lo : lo + n],
                        MULT,
                    )
            for at in range(0, n, P):
                token_terms[half, lo + at] = terms[:, :, :, at : at + P]
            return terms

        def add_terms(result, terms):
            nc.vector.tensor_tensor(result, terms[:, 0], terms[:, 1], ADD)

        def store_result(result, half, lo, n):
            rows = out_0[half * PIECE : (half + 1) * PIECE, lo : lo + n]
            nc.sync.dma_start(out=rows.rearrange("(b q) t -> q b t", q=P), in_=result)

        def turn_to_tokens(half, i):
            lo, n = TOKEN_CHUNKS[i]
            acc = bank(2 + 2 * half + i % 2)
            for kk in range(n // P):
                terms = token_terms[half, lo + kk * P]
                for b in range(BLOCKS):
                    at = (kk * BLOCKS + b) * P
                    for r in range(2):
                        nc.tensor.matmul(
                            acc[:, at : at + P], terms[:, r, b, :], ident[:], is_transpose=True, start=(r == 0), stop=(r == 1)
                        )
            nc.scalar.copy(
                out=by_token[i][:, :, :, 64 * half : 64 * (half + 1), :],
                in_=acc[:, 0 : n * BLOCKS].rearrange("k (kk p u e) -> k kk u p e", p=64, u=2, e=PAIR),
            )

        def turn_back(i):
            lo, n = TOKEN_CHUNKS[i]
            acc = bank(6 + i % 2)
            words = by_token[i][:].rearrange("k kk u p e -> k (kk u p e)").bitcast(F32)
            for at in range(0, 2 * n, P):
                nc.tensor.transpose(acc[:, at : at + P], words[:, at : at + P], ident[:])
            rounded = ringed("rounded", [P, n * PACK], BF16, 2)
            nc.scalar.copy(
                out=rounded[:].bitcast(F32).rearrange("p (kk r u) -> p kk r u", r=P, u=2),
                in_=acc[:, 0 : 2 * n].rearrange("p (kk u r) -> p kk r u", r=P, u=2),
            )
            nc.vector.quantize_mx(
                out=out_codes[:, lo : lo + n].bitcast(FP8X4), scales=out_scales[:, lo : lo + n], in_=rounded[:]
            )
            nc.sync.dma_start(
                out=out_1[0].rearrange("p t d -> p (t d)").bitcast(I32)[:, lo : lo + n],
                in_=out_codes[:, lo : lo + n].bitcast(I32),
            )

        duos = []
        picked = gather_run(0)
        for d, (first, count) in enumerate(EXPERT_RUNS):
            woven = weave_run(d, picked)
            if d + 1 < len(EXPERT_RUNS):
                picked = gather_run(d + 1)
            quantise_run(d, woven)
            for e in range(first, first + count, 2):
                duos.append(w2_duo(0, e))
                if e == 0:
                    early_duo = w2_duo(1, 0)
            expert_run(0, d, duos)

        duos = [early_duo]
        for d, (first, count) in enumerate(EXPERT_RUNS):
            for e in range(max(first, 2), first + count, 2):
                duos.append(w2_duo(1, e))
                if e == 2:
                    early = [gated_terms(held("early_terms", [P, 2, BLOCKS, EARLY_CHUNKS[0][1]], F32), 0, *EARLY_CHUNKS[0])]
            expert_run(1, d, duos)
        early.append(gated_terms(held("last_duo", [P, 2, BLOCKS, EARLY_CHUNKS[1][1]], F32), 0, *EARLY_CHUNKS[1]))
        result = held("early_result", [P, BLOCKS, EARLY_CHUNKS[1][1]], F32)
        add_terms(result[:], early[1])
        store_result(result[:], 0, *EARLY_CHUNKS[1])
        for i in range(len(TOKEN_CHUNKS)):
            turn_to_tokens(0, i)

        for i, (lo, n) in enumerate(TOKEN_CHUNKS):
            terms = gated_terms(ringed("terms", [P, 2, BLOCKS, n], F32, 2), 1, lo, n)
            turn_to_tokens(1, i)
            result = held("result%d" % i, [P, BLOCKS, n], F32)
            add_terms(result[:], terms)
            store_result(result[:], 1, lo, n)
            turn_back(i)
        result = held("y3", [P, BLOCKS, EARLY_CHUNKS[0][1]], F32)
        for lo, n in TOKEN_CHUNKS[:2]:
            add_terms(result[:, :, lo : lo + n], early[0][:, :, :, lo : lo + n])
            store_result(result[:, :, lo : lo + n], 0, lo, n)
        for q in range(4):
            queue = nc.sync if q % 2 == 0 else nc.scalar
            queue.dma_start(
                out=out_2[0, 4 * q : 4 * q + 4, :].bitcast(I32), in_=out_scales[32 * q : 32 * q + 4, :].bitcast(I32)
            )
